import numpy as np
import ml_dtypes


def mxq(x, axis, fmt="e4m3"):
    dtype, down = {"e4m3": (ml_dtypes.float8_e4m3fn, 7), "e5m2": (ml_dtypes.float8_e5m2, 14)}[fmt]
    v = np.moveaxis(np.asarray(x, np.float32).astype(ml_dtypes.bfloat16).astype(np.float64), axis, -1)
    blocks = v.reshape(v.shape[:-1] + (-1, 32))
    amax = np.abs(blocks).max(-1, keepdims=True)
    byte = np.maximum(np.where(amax > 0, np.frexp(amax)[1] - 1 + 127, 0) - down, 1)
    scale = np.exp2(byte - 127.0)
    codes = (blocks / scale).astype(np.float32).astype(dtype).astype(np.float64)
    return np.moveaxis((codes * scale).reshape(v.shape), -1, axis)


WIDE = False


def mx_kscale(k):
    if not WIDE:
        return np.ones(k)
    levels = np.array([10, -10, 5, -5, 0])
    if k % 512:
        return np.exp2(np.random.permutation(np.resize(levels, k // 32))).repeat(32)
    a = np.empty((k // 512, 16))
    for p in range(k // 512):
        a[p, :8] = np.random.permutation(np.resize(levels, 8))
        for g in range(8):
            far = levels[np.abs(levels - a[p, g]) >= 10]
            a[p, g + 8] = far[np.random.randint(len(far))]
    return np.exp2(a.ravel()).repeat(32)


def f64(x):
    return np.asarray(x).astype(np.float64)


def striped(idx):
    return np.tile(idx.reshape(-1, 16).T, (8, 1)).astype(np.uint16)


def unstriped(offs):
    return offs[:16].T.reshape(-1).astype(np.int64)


def striped8(idx):
    return np.concatenate([x.reshape(-1, 16).T for x in idx]).astype(np.uint16)


def runs(offs, k):
    lists = np.stack([offs[16 * r : 16 * r + 16].T.reshape(-1) for r in range(8)]).astype(np.int64)
    return lists[np.arange(k) % 512 // 64]


def pack_weight(w):
    k, n = w.shape
    w = f64(np.asarray(w, np.float32).astype(ml_dtypes.bfloat16)).reshape(k // 32, 32, n)
    amax = np.abs(w).max(1)
    byte = np.clip(np.where(amax > 0, np.frexp(amax)[1] - 1 + 127 - 7, 1), 1, 254)
    scaled = (w * np.exp2(127.0 - byte)[:, None, :]).reshape(k, n).astype(np.float32)
    words = np.ascontiguousarray(scaled.reshape(k // 512, 128, 4, n).transpose(0, 1, 3, 2)).astype(ml_dtypes.float8_e4m3fn).view(np.uint8)
    return words, np.ascontiguousarray(byte.astype(np.uint8).reshape(k // 512, 16, n))


def unpack_weight(words, scales):
    g, p, n, _ = words.shape
    vals = np.ascontiguousarray(words).view(ml_dtypes.float8_e4m3fn).astype(np.float64) * np.repeat(np.exp2(scales.astype(np.float64) - 127.0), 8, axis=1)[..., None]
    return vals.transpose(0, 1, 3, 2).reshape(g * 512, n)


E2M1 = np.array([0.0, 0.5, 1.0, 1.5, 2.0, 3.0, 4.0, 6.0, -0.0, -0.5, -1.0, -1.5, -2.0, -3.0, -4.0, -6.0])


def pack_fp4(w):
    k, n = w.shape
    w = f64(np.asarray(w, np.float32).astype(ml_dtypes.bfloat16)).reshape(k // 32, 32, n)
    amax = np.abs(w).max(1)
    mant, ex = np.frexp(amax / 6.0)
    byte = np.clip(np.where(amax > 0, np.where(mant > 0.5, ex, ex - 1) + 127, 1), 1, 254)
    scaled = (w * np.exp2(127.0 - byte)[:, None, :]).reshape(k, n).astype(np.float32)
    c = np.ascontiguousarray(scaled.reshape(k // 512, 128, 4, n).transpose(0, 1, 3, 2)).astype(ml_dtypes.float4_e2m1fn).view(np.uint8) & 0xF
    words = (c[..., 0::2] | (c[..., 1::2] << 4)).reshape(k // 512, 128, 2 * n)
    return np.ascontiguousarray(words), np.ascontiguousarray(byte.astype(np.uint8).reshape(k // 512, 16, n))


def unpack_fp4(words, scales):
    g, _, n = scales.shape
    words = np.ascontiguousarray(words).reshape(g, 128, n, 2)
    nib = np.empty((g, 128, n, 4), np.uint8)
    nib[..., 0::2] = words & 0xF
    nib[..., 1::2] = words >> 4
    vals = E2M1[nib] * np.repeat(np.exp2(scales.astype(np.float64) - 127.0), 8, axis=1)[..., None]
    return vals.transpose(0, 1, 3, 2).reshape(g * 512, n)


def planes(y):
    n, m = y.shape
    v = y.astype(np.float32).astype(ml_dtypes.bfloat16).astype(np.float64).reshape(n // 32, 32, m)
    top = np.abs(v).max(1)
    byte = np.clip(np.where(top > 0, np.frexp(top)[1] - 1 + 127 - 7, 1), 1, 254)
    codes = (v * np.exp2(127.0 - byte)[:, None, :]).reshape(n, m).astype(np.float32).astype(ml_dtypes.float8_e4m3fn).view(np.uint8)
    words = codes.reshape(n // 512, 128, 4, m).transpose(0, 1, 3, 2)
    return np.ascontiguousarray(words), np.ascontiguousarray(byte.astype(np.uint8).reshape(n // 512, 16, m))


K, T, S, N, H = 512, 2048, 512, 512, 512


def setup_inputs():
    n = np.random.standard_normal
    s = mx_kscale(K)[:, None]
    u = mx_kscale(H)
    packed_xT = pack_weight(n((K, T)) * s)
    packed_w1 = pack_fp4(n((K, H)) / np.sqrt(K) / s)
    packed_w2 = pack_fp4(n((H, N)) / np.sqrt(H) / u[:, None])
    return {
        "x_words": packed_xT[0],
        "x_scales": packed_xT[1],
        "w1_words": packed_w1[0],
        "w1_scales": packed_w1[1],
        "gn": (np.random.uniform(0.5, 1.5, (H, 1)) * u[:, None]).astype(np.float32),
        "w2_words": packed_w2[0],
        "w2_scales": packed_w2[1],
        "offs": striped(np.random.permutation(T)[:S]),
        "n1": striped8(np.stack([np.random.permutation(S) for _ in range(8)])),
        "n2": striped8(np.stack([np.random.permutation(S) for _ in range(8)])),
        "n3": striped8(np.stack([np.random.permutation(S) for _ in range(8)])),
        "n4": striped8(np.stack([np.random.permutation(S) for _ in range(8)])),
    }


def reference(x_words, x_scales, w1_words, w1_scales, gn, w2_words, w2_scales, offs, n1, n2, n3, n4):
    xq = unpack_weight(x_words, x_scales)[:, unstriped(offs)]
    y = unpack_fp4(w1_words, w1_scales).T @ xq
    st = y + 0.5 * (y[np.arange(H)[:, None], runs(n1, H)])
    z = f64(gn) * (st - (st[np.arange(H)[:, None], runs(n2, H)]))
    h = unpack_fp4(w2_words, w2_scales).T @ mxq(z, 0, "e4m3")
    out_0 = h * (h[np.arange(N)[:, None], runs(n3, N)] - (h[np.arange(N)[:, None], runs(n4, N)]))
    return (out_0,) + planes(out_0)

@@ -1,0 +1,191 @@
+from contextlib import ExitStack
+
+import concourse.mybir as mybir
+
+K, T, S, H, N = 512, 2048, 512, 512, 512
+FLOPS = 2 * K * H * S + 2 * H * N * S
+
+F32 = mybir.dt.float32
+BF16 = mybir.dt.bfloat16
+I32 = mybir.dt.int32
+U32 = mybir.dt.uint32
+U16 = mybir.dt.uint16
+U8 = mybir.dt.uint8
+FP8X4 = mybir.dt.float8_e4m3fn_x4
+FP4X4 = mybir.dt.float4_e2m1fn_x4
+ALU = mybir.AluOpType
+COPY = mybir.ActivationFunctionType.Copy
+
+P = 128
+PACK = 4
+HALVES = [(0, 256), (256, 512)]
+CHUNKS = [(0, 256), (256, 384), (384, 512)]
+
+
+def tile_picked_layhopwind_none_po_kernel(tc, x_words, x_scales, w1_words, w1_scales, gn, w2_words, w2_scales, offs, n1, n2, n3, n4, out_0, out_1, out_2):
+    nc = tc.nc
+    with ExitStack() as ctx:
+        keep = ctx.enter_context(tc.tile_pool(name="keep", bufs=1))
+        psum = ctx.enter_context(tc.psum_pool(name="psum", bufs=1))
+
+        def sb(name, shape, dtype):
+            return keep.tile(shape, dtype, name=name, align_bytes=64)
+
+        def bank(b):
+            return psum.tile([P, 512], F32, name=f"bank{b}")
+
+        def entries(lst, lo, hi):
+            return lst[:, lo // 16 : hi // 16]
+
+        def load_scale_rows(queue, tile, src, quads):
+            for q in quads:
+                queue.dma_start(out=tile[32 * q : 32 * q + 4, :].bitcast(I32), in_=src[0, 4 * q : 4 * q + 4, :].bitcast(I32))
+
+        offs_sb = keep.tile([P, S // 16], U16, name="offs_sb")
+        n1_sb = keep.tile([P, S // 16], U16, name="n1_sb")
+        n2_sb = keep.tile([P, S // 16], U16, name="n2_sb")
+        n3_sb = keep.tile([P, S // 16], U16, name="n3_sb")
+        n4_sb = keep.tile([P, S // 16], U16, name="n4_sb")
+
+        xw = sb("xw", [P, T], I32)
+        xs = sb("xs", [P, T], U8)
+        ww = sb("ww", [P, 2 * H], U8)
+        ws = sb("ws", [P, H], U8)
+        gain = sb("gain", [P, PACK], F32)
+        gain2 = sb("gain2", [P, PACK], F32)
+
+        nc.gpsimd.memset(xs[:].bitcast(I32), 0)
+        nc.gpsimd.memset(ws[:].bitcast(I32), 0)
+
+        nc.sync.dma_start(offs_sb[:], offs)
+        nc.scalar.dma_start(out=ww[:].bitcast(I32), in_=w1_words[0].bitcast(I32))
+        nc.sync.dma_start(n1_sb[:], n1)
+        nc.scalar.dma_start(out=xw[:], in_=x_words[0].rearrange("p n r -> p (n r)").bitcast(I32))
+        load_scale_rows(nc.sync, xs, x_scales, range(4))
+        load_scale_rows(nc.sync, ws, w1_scales, range(2))
+        load_scale_rows(nc.gpsimd, ws, w1_scales, range(2, 4))
+        nc.sync.dma_start(out=gain[:], in_=gn.rearrange("(p t) o -> p (t o)", t=PACK))
+        nc.sync.dma_start(n2_sb[:], n2)
+        nc.sync.dma_start(n3_sb[:], n3)
+        nc.sync.dma_start(n4_sb[:], n4)
+
+        nc.scalar.activation(gain2[:], gain[:], COPY, scale=2.0)
+
+        def deal(name, words, scales, t0, t1):
+            n = t1 - t0
+            dw = sb(name + "w", [P, n * 2 * P], U8)
+            ds = sb(name + "s", [P, n * P], U8)
+            nc.vector.tensor_copy(
+                out=dw[:].rearrange("p (t m b) -> p t m b", t=n, b=2),
+                in_=words[:].rearrange("p (m t b) -> p t m b", t=PACK, b=2)[:, t0:t1],
+            )
+            nc.vector.tensor_copy(
+                out=ds[:].rearrange("p (t m) -> p t m", t=n),
+                in_=scales[:].rearrange("p (m t) -> p t m", t=PACK)[:, t0:t1],
+            )
+            return [(dw[:, 2 * P * i : 2 * P * (i + 1)].bitcast(FP4X4), ds[:, P * i : P * (i + 1)]) for i in range(n)]
+
+        def product(dst, weight, words, scales):
+            nc.tensor.matmul_mx(out=dst, lhsT=weight[0], lhsT_scale=weight[1], rhs=words.bitcast(FP8X4), rhs_scale=scales, start=True, stop=True)
+
+        def interleave(engine_is_vector, dst, src, scale):
+            o = dst[:].rearrange("p (c i t) -> p c t i", i=4, t=PACK)
+            i = src[:].rearrange("p t (c i) -> p c t i", i=4)
+            if engine_is_vector:
+                if scale == 1.0:
+                    nc.vector.tensor_copy(out=o, in_=i)
+                else:
+                    nc.vector.tensor_scalar(o, i, scale, None, op0=ALU.mult)
+            else:
+                nc.scalar.activation(o, i, COPY, scale=scale)
+
+        xgs = sb("xgs", [P, S], U8)
+        xgw = sb("xgw", [P, S], U32)
+        nc.vector.tensor_copy(xgs[:], xs[:].indirect(offs_sb[:]))
+        w1 = deal("w1a", ww, ws, 0, 1)
+        for lo, hi in HALVES:
+            nc.vector.tensor_copy(xgw[:, lo:hi], xw[:].bitcast(U32).indirect(entries(offs_sb, lo, hi)))
+        w1 = w1 + deal("w1b", ww, ws, 1, PACK)
+        nc.sync.dma_start(out=ww[:].bitcast(I32), in_=w2_words[0].bitcast(I32))
+        load_scale_rows(nc.sync, ws, w2_scales, range(4))
+
+        gy = [sb(f"gy{t}", [P, S], F32) for t in range(PACK)]
+        gy2 = [sb(f"gy2{t}", [P, S], F32) for t in range(PACK)]
+        st = [sb(f"st{t}", [P, S], F32) for t in range(PACK)]
+        stc = [sb(f"stc{t}", [P, S], F32) for t in range(PACK)]
+
+        nb = 0
+        for t in range(PACK):
+            for lo, hi in (HALVES if t == 0 else [(0, S)]):
+                acc = bank(nb)
+                nb = nb + 1
+                product(acc[:, : hi - lo], w1[t], xgw[:, lo:hi], xgs[:, lo:hi])
+                nc.scalar.activation(gy[t][:, lo:hi], acc[:, : hi - lo], COPY, scale=gain[:, t : t + 1])
+                nc.scalar.activation(gy2[t][:, lo:hi], acc[:, : hi - lo], COPY, scale=gain2[:, t : t + 1])
+            for lo, hi in HALVES:
+                nc.vector.tensor_tensor(st[t][:, lo:hi], gy[t][:].indirect(entries(n1_sb, lo, hi)), gy2[t][:, lo:hi], ALU.add)
+        for t in range(PACK):
+            nc.scalar.copy(stc[t][:], st[t][:])
+
+        w2 = deal("w2a", ww, ws, 0, 2)
+        zw = sb("zw", [P, S], U32)
+        zs = sb("zs", [P, S], U8)
+        h = [sb(f"h{t}", [P, S], F32) for t in range(PACK)]
+        early = [bank(5), bank(6)]
+        pending = None
+        for c, (lo, hi) in enumerate(CHUNKS):
+            dz = sb(f"dz{c}", [P, PACK, hi - lo], F32)
+            zb = sb(f"zb{c}", [P, PACK * (hi - lo)], BF16)
+            for t in range(PACK):
+                nc.vector.tensor_tensor(dz[:, t, :], st[t][:].indirect(entries(n2_sb, lo, hi)), stc[t][:, lo:hi], ALU.subtract)
+            if pending is not None:
+                plo, phi, pzb = pending
+                nc.vector.quantize_mx(out=zw[:, plo:phi].bitcast(FP8X4), scales=zs[:, plo:phi], in_=pzb[:])
+                for t in range(2):
+                    product(early[t][:, plo:phi], w2[t], zw[:, plo:phi], zs[:, plo:phi])
+            interleave(c == len(CHUNKS) - 1, zb, dz, -0.5)
+            pending = (lo, hi, zb)
+        lo, hi, zb = pending
+        nc.vector.quantize_mx(out=zw[:, lo:hi].bitcast(FP8X4), scales=zs[:, lo:hi], in_=zb[:])
+        w2 = w2 + deal("w2b", ww, ws, 2, PACK)
+        for t in range(2):
+            nc.scalar.copy(h[t][:, :lo], early[t][:, :lo])
+        for t in range(2):
+            acc = bank(t)
+            product(acc[:, lo:hi], w2[t], zw[:, lo:hi], zs[:, lo:hi])
+            nc.scalar.copy(h[t][:, lo:hi], acc[:, lo:hi])
+        for t in range(2, PACK):
+            acc = bank(t)
+            product(acc[:], w2[t], zw[:], zs[:])
+            nc.scalar.copy(h[t][:], acc[:])
+
+        ow = sb("ow", [P, S], U32)
+        osc = sb("osc", [P, S], U8)
+        out_rows = out_0.rearrange("(p t) j -> p t j", t=PACK)
+        out_words = out_1[0].rearrange("p n r -> p (n r)").bitcast(I32)
+        pending = None
+        for c, (lo, hi) in enumerate(CHUNKS):
+            g4 = sb(f"g4{c}", [P, PACK, hi - lo], F32)
+            dd = sb(f"dd{c}", [P, PACK, hi - lo], F32)
+            res = sb(f"res{c}", [P, PACK, hi - lo], F32)
+            ob = sb(f"ob{c}", [P, PACK * (hi - lo)], BF16)
+            for pair in ((0, 1), (2, 3)):
+                for t in pair:
+                    nc.vector.tensor_copy(g4[:, t, :], h[t][:].indirect(entries(n4_sb, lo, hi)))
+                for t in pair:
+                    nc.vector.tensor_tensor(dd[:, t, :], h[t][:].indirect(entries(n3_sb, lo, hi)), g4[:, t, :], ALU.subtract)
+                if pending is not None and pair[0] == 2:
+                    plo, phi, pob = pending
+                    nc.vector.quantize_mx(out=ow[:, plo:phi].bitcast(FP8X4), scales=osc[:, plo:phi], in_=pob[:])
+                    nc.sync.dma_start(out=out_words[:, plo:phi], in_=ow[:, plo:phi].bitcast(I32))
+                for t in pair:
+                    nc.vector.tensor_tensor(res[:, t, :], dd[:, t, :], h[t][:, lo:hi], ALU.mult)
+            nc.sync.dma_start(out=out_rows[:, :, lo:hi], in_=res[:])
+            interleave(c == len(CHUNKS) - 1, ob, res, 1.0)
+            pending = (lo, hi, ob)
+        lo, hi, ob = pending
+        nc.vector.quantize_mx(out=ow[:, lo:hi].bitcast(FP8X4), scales=osc[:, lo:hi], in_=ob[:])
+        nc.sync.dma_start(out=out_words[:, lo:hi], in_=ow[:, lo:hi].bitcast(I32))
+        for q in range(4):
+            queue = nc.scalar if q < 2 else nc.sync
+            queue.dma_start(out=out_2[0, 4 * q : 4 * q + 4, :].bitcast(I32), in_=osc[32 * q : 32 * q + 4, :].bitcast(I32))

@@ -28,8 +28,8 @@ def tile_picked_layhopwind_none_po_kernel(tc, x_words, x_scales, w1_words, w1_sc
         keep = ctx.enter_context(tc.tile_pool(name="keep", bufs=1))
         psum = ctx.enter_context(tc.psum_pool(name="psum", bufs=1))
 
-        def sb(name, shape, dtype):
-            return keep.tile(shape, dtype, name=name, align_bytes=64)
+        def sb(name, shape, dtype, tag=None):
+            return keep.tile(shape, dtype, name=name, tag=tag or name, align_bytes=64)
 
         def bank(b):
             return psum.tile([P, 512], F32, name=f"bank{b}")
@@ -69,17 +69,17 @@ def tile_picked_layhopwind_none_po_kernel(tc, x_words, x_scales, w1_words, w1_sc
         nc.sync.dma_start(n3_sb[:], n3)
         nc.sync.dma_start(n4_sb[:], n4)
 
-        nc.scalar.activation(gain2[:], gain[:], COPY, scale=2.0)
+        nc.scalar.activation(gain2[:], gain[:], COPY, scale=0.5)
 
-        def deal(name, words, scales, t0, t1):
+        def deal(engine, name, words, scales, t0, t1):
             n = t1 - t0
             dw = sb(name + "w", [P, n * 2 * P], U8)
             ds = sb(name + "s", [P, n * P], U8)
-            nc.vector.tensor_copy(
+            engine.tensor_copy(
                 out=dw[:].rearrange("p (t m b) -> p t m b", t=n, b=2),
                 in_=words[:].rearrange("p (m t b) -> p t m b", t=PACK, b=2)[:, t0:t1],
             )
-            nc.vector.tensor_copy(
+            engine.tensor_copy(
                 out=ds[:].rearrange("p (t m) -> p t m", t=n),
                 in_=scales[:].rearrange("p (m t) -> p t m", t=PACK)[:, t0:t1],
             )
@@ -89,8 +89,8 @@ def tile_picked_layhopwind_none_po_kernel(tc, x_words, x_scales, w1_words, w1_sc
             nc.tensor.matmul_mx(out=dst, lhsT=weight[0], lhsT_scale=weight[1], rhs=words.bitcast(FP8X4), rhs_scale=scales, start=True, stop=True)
 
         def interleave(engine_is_vector, dst, src, scale):
-            o = dst[:].rearrange("p (c i t) -> p c t i", i=4, t=PACK)
-            i = src[:].rearrange("p t (c i) -> p c t i", i=4)
+            o = dst.rearrange("p (c i t) -> p c t i", i=4, t=PACK)
+            i = src.rearrange("p t (c i) -> p c t i", i=4)
             if engine_is_vector:
                 if scale == 1.0:
                     nc.vector.tensor_copy(out=o, in_=i)
@@ -100,60 +100,61 @@ def tile_picked_layhopwind_none_po_kernel(tc, x_words, x_scales, w1_words, w1_sc
                 nc.scalar.activation(o, i, COPY, scale=scale)
 
         xgs = sb("xgs", [P, S], U8)
-        xgw = sb("xgw", [P, S], U32)
+        xgw = sb("xgw", [P, S], U32, tag="xs")
         nc.vector.tensor_copy(xgs[:], xs[:].indirect(offs_sb[:]))
-        w1 = deal("w1a", ww, ws, 0, 1)
+        w1 = deal(nc.gpsimd, "w1a", ww, ws, 0, 1)
         for lo, hi in HALVES:
             nc.vector.tensor_copy(xgw[:, lo:hi], xw[:].bitcast(U32).indirect(entries(offs_sb, lo, hi)))
-        w1 = w1 + deal("w1b", ww, ws, 1, PACK)
+        w1 = w1 + deal(nc.gpsimd, "w1b", ww, ws, 1, PACK)
         nc.sync.dma_start(out=ww[:].bitcast(I32), in_=w2_words[0].bitcast(I32))
         load_scale_rows(nc.sync, ws, w2_scales, range(4))
 
-        gy = [sb(f"gy{t}", [P, S], F32) for t in range(PACK)]
-        gy2 = [sb(f"gy2{t}", [P, S], F32) for t in range(PACK)]
-        st = [sb(f"st{t}", [P, S], F32) for t in range(PACK)]
-        stc = [sb(f"stc{t}", [P, S], F32) for t in range(PACK)]
+        win = [sb(f"win{t}", [P, S if t == 0 else 2 * S], F32) for t in range(PACK)]
+        st = [sb(f"st{t}", [P, 2 * S if t < 2 else S], F32) for t in range(PACK)]
+        gy = [win[t + 1][:, S:] for t in range(PACK - 1)] + [st[0][:, S:]]
+        stc = [st[1][:, S:]] + [sb(f"stc{t}", [P, S], F32)[:] for t in range(1, PACK)]
+        pieces = [(0, 0, S), (1, 0, S)] + [(t, lo, hi) for lo, hi in HALVES for t in (2, 3)]
 
         nb = 0
         for t in range(PACK):
-            for lo, hi in (HALVES if t == 0 else [(0, S)]):
+            parts = HALVES if t == 0 else [(0, S)]
+            for lo, hi in parts:
                 acc = bank(nb)
                 nb = nb + 1
                 product(acc[:, : hi - lo], w1[t], xgw[:, lo:hi], xgs[:, lo:hi])
-                nc.scalar.activation(gy[t][:, lo:hi], acc[:, : hi - lo], COPY, scale=gain[:, t : t + 1])
-                nc.scalar.activation(gy2[t][:, lo:hi], acc[:, : hi - lo], COPY, scale=gain2[:, t : t + 1])
-            for lo, hi in HALVES:
-                nc.vector.tensor_tensor(st[t][:, lo:hi], gy[t][:].indirect(entries(n1_sb, lo, hi)), gy2[t][:, lo:hi], ALU.add)
-        for t in range(PACK):
-            nc.scalar.copy(stc[t][:], st[t][:])
+                if lo == 0:
+                    nc.scalar.activation(win[t][:, lo:hi], acc[:, : hi - lo], COPY, scale=gain2[:, t : t + 1])
+                    nc.scalar.activation(gy[t][:, lo:hi], acc[:, : hi - lo], COPY, scale=gain[:, t : t + 1])
+                else:
+                    nc.vector.tensor_scalar(win[t][:, lo:hi], acc[:, : hi - lo], gain2[:, t : t + 1], None, op0=ALU.mult)
+                    nc.vector.tensor_scalar(gy[t][:, lo:hi], acc[:, : hi - lo], gain[:, t : t + 1], None, op0=ALU.mult)
+            for lo, hi in parts:
+                nc.vector.tensor_tensor(st[t][:, lo:hi], win[t][:].indirect(entries(n1_sb, lo, hi)), gy[t][:, lo:hi], ALU.add)
+        for t, lo, hi in pieces:
+            nc.scalar.copy(stc[t][:, lo:hi], st[t][:, lo:hi])
 
-        w2 = deal("w2a", ww, ws, 0, 2)
+        def round_and_interleave(dst, src, lo, hi, scale, split):
+            mid = (lo + hi) // 2 if split else hi
+            interleave(False, dst[:, : PACK * (mid - lo)], src[:, :, lo:mid], scale)
+            if split:
+                interleave(True, dst[:, PACK * (mid - lo) :], src[:, :, mid:hi], scale)
+
+        w2 = deal(nc.vector, "w2a", ww, ws, 0, 2)
         zw = sb("zw", [P, S], U32)
         zs = sb("zs", [P, S], U8)
-        h = [sb(f"h{t}", [P, S], F32) for t in range(PACK)]
-        early = [bank(5), bank(6)]
-        pending = None
-        for c, (lo, hi) in enumerate(CHUNKS):
-            dz = sb(f"dz{c}", [P, PACK, hi - lo], F32)
+        h = [win[1], win[2], sb("h2", [P, S], F32), sb("h3", [P, S], F32)]
+        dz = sb("dz", [P, PACK, S], F32)
+        for t, lo, hi in pieces:
+            nc.vector.tensor_tensor(dz[:, t, lo:hi], st[t][:].indirect(entries(n2_sb, lo, hi)), stc[t][:, lo:hi], ALU.subtract)
+        for c, (lo, hi) in enumerate(HALVES):
             zb = sb(f"zb{c}", [P, PACK * (hi - lo)], BF16)
-            for t in range(PACK):
-                nc.vector.tensor_tensor(dz[:, t, :], st[t][:].indirect(entries(n2_sb, lo, hi)), stc[t][:, lo:hi], ALU.subtract)
-            if pending is not None:
-                plo, phi, pzb = pending
-                nc.vector.quantize_mx(out=zw[:, plo:phi].bitcast(FP8X4), scales=zs[:, plo:phi], in_=pzb[:])
-                for t in range(2):
-                    product(early[t][:, plo:phi], w2[t], zw[:, plo:phi], zs[:, plo:phi])
-            interleave(c == len(CHUNKS) - 1, zb, dz, -0.5)
-            pending = (lo, hi, zb)
-        lo, hi, zb = pending
-        nc.vector.quantize_mx(out=zw[:, lo:hi].bitcast(FP8X4), scales=zs[:, lo:hi], in_=zb[:])
-        w2 = w2 + deal("w2b", ww, ws, 2, PACK)
-        for t in range(2):
-            nc.scalar.copy(h[t][:, :lo], early[t][:, :lo])
-        for t in range(2):
-            acc = bank(t)
-            product(acc[:, lo:hi], w2[t], zw[:, lo:hi], zs[:, lo:hi])
-            nc.scalar.copy(h[t][:, lo:hi], acc[:, lo:hi])
+            round_and_interleave(zb, dz, lo, hi, -1.0, c == 1)
+            nc.vector.quantize_mx(out=zw[:, lo:hi].bitcast(FP8X4), scales=zs[:, lo:hi], in_=zb[:])
+            for t in range(2):
+                acc = bank(5 + t if c == 0 else t)
+                product(acc[:, lo:hi], w2[t], zw[:, lo:hi], zs[:, lo:hi])
+                nc.scalar.copy(h[t][:, lo:hi], acc[:, lo:hi])
+        w2 = w2 + deal(nc.vector, "w2b", ww, ws, 2, PACK)
         for t in range(2, PACK):
             acc = bank(t)
             product(acc[:], w2[t], zw[:], zs[:])
@@ -163,29 +164,31 @@ def tile_picked_layhopwind_none_po_kernel(tc, x_words, x_scales, w1_words, w1_sc
         osc = sb("osc", [P, S], U8)
         out_rows = out_0.rearrange("(p t) j -> p t j", t=PACK)
         out_words = out_1[0].rearrange("p n r -> p (n r)").bitcast(I32)
-        pending = None
-        for c, (lo, hi) in enumerate(CHUNKS):
-            g4 = sb(f"g4{c}", [P, PACK, hi - lo], F32)
-            dd = sb(f"dd{c}", [P, PACK, hi - lo], F32)
-            res = sb(f"res{c}", [P, PACK, hi - lo], F32)
-            ob = sb(f"ob{c}", [P, PACK * (hi - lo)], BF16)
-            for pair in ((0, 1), (2, 3)):
-                for t in pair:
-                    nc.vector.tensor_copy(g4[:, t, :], h[t][:].indirect(entries(n4_sb, lo, hi)))
-                for t in pair:
-                    nc.vector.tensor_tensor(dd[:, t, :], h[t][:].indirect(entries(n3_sb, lo, hi)), g4[:, t, :], ALU.subtract)
-                if pending is not None and pair[0] == 2:
-                    plo, phi, pob = pending
-                    nc.vector.quantize_mx(out=ow[:, plo:phi].bitcast(FP8X4), scales=osc[:, plo:phi], in_=pob[:])
-                    nc.sync.dma_start(out=out_words[:, plo:phi], in_=ow[:, plo:phi].bitcast(I32))
-                for t in pair:
-                    nc.vector.tensor_tensor(res[:, t, :], dd[:, t, :], h[t][:, lo:hi], ALU.mult)
-            nc.sync.dma_start(out=out_rows[:, :, lo:hi], in_=res[:])
-            interleave(c == len(CHUNKS) - 1, ob, res, 1.0)
-            pending = (lo, hi, ob)
-        lo, hi, ob = pending
-        nc.vector.quantize_mx(out=ow[:, lo:hi].bitcast(FP8X4), scales=osc[:, lo:hi], in_=ob[:])
-        nc.sync.dma_start(out=out_words[:, lo:hi], in_=ow[:, lo:hi].bitcast(I32))
+        g4 = sb("g4", [P, PACK, S], F32)
+        dd = sb("dd", [P, PACK, S], F32)
+        res = sb("res", [P, PACK, S], F32)
+        ob = [sb(f"ob{c}", [P, PACK * (hi - lo)], BF16) for c, (lo, hi) in enumerate(HALVES)]
+
+        def quantise_out(c):
+            lo, hi = HALVES[c]
+            nc.vector.quantize_mx(out=ow[:, lo:hi].bitcast(FP8X4), scales=osc[:, lo:hi], in_=ob[c][:])
+            nc.sync.dma_start(out=out_words[:, lo:hi], in_=ow[:, lo:hi].bitcast(I32))
+
+        for i in range(0, len(pieces), 2):
+            pair = pieces[i : i + 2]
+            for t, lo, hi in pair:
+                nc.vector.tensor_copy(g4[:, t, lo:hi], h[t][:].indirect(entries(n4_sb, lo, hi)))
+            for t, lo, hi in pair:
+                nc.vector.tensor_tensor(dd[:, t, lo:hi], h[t][:].indirect(entries(n3_sb, lo, hi)), g4[:, t, lo:hi], ALU.subtract)
+            if i == 4:
+                quantise_out(0)
+            for t, lo, hi in pair:
+                nc.vector.tensor_tensor(res[:, t, lo:hi], dd[:, t, lo:hi], h[t][:, lo:hi], ALU.mult)
+            t0, lo, hi = pair[0]
+            nc.sync.dma_start(out=out_rows[:, t0 : t0 + 2, lo:hi], in_=res[:, t0 : t0 + 2, lo:hi])
+            if i > 0:
+                round_and_interleave(ob[i // 2 - 1], res, lo, hi, 1.0, i == 4)
+        quantise_out(1)
         for q in range(4):
             queue = nc.scalar if q < 2 else nc.sync
             queue.dma_start(out=out_2[0, 4 * q : 4 * q + 4, :].bitcast(I32), in_=osc[32 * q : 32 * q + 4, :].bitcast(I32))

@@ -54,27 +54,29 @@ def tile_picked_layhopwind_none_po_kernel(tc, x_words, x_scales, w1_words, w1_sc
         gain = sb("gain", [P, PACK], F32)
         gain2 = sb("gain2", [P, PACK], F32)
 
-        nc.gpsimd.memset(xs[:].bitcast(I32), 0)
+        nc.vector.memset(xs[:, : T // 2].bitcast(I32), 0)
+        nc.gpsimd.memset(xs[:, T // 2 :].bitcast(I32), 0)
         nc.gpsimd.memset(ws[:].bitcast(I32), 0)
 
-        nc.sync.dma_start(offs_sb[:], offs)
+        x_rows = x_words[0].rearrange("p n r -> p (n r)").bitcast(I32)
+        nc.sync.dma_start(out=xw[:, :512], in_=x_rows[:, :512])
         nc.scalar.dma_start(out=ww[:].bitcast(I32), in_=w1_words[0].bitcast(I32))
-        nc.sync.dma_start(n1_sb[:], n1)
-        nc.scalar.dma_start(out=xw[:], in_=x_words[0].rearrange("p n r -> p (n r)").bitcast(I32))
+        nc.sync.dma_start(offs_sb[:], offs)
         load_scale_rows(nc.sync, xs, x_scales, range(4))
-        load_scale_rows(nc.sync, ws, w1_scales, range(2))
-        load_scale_rows(nc.gpsimd, ws, w1_scales, range(2, 4))
+        nc.sync.dma_start(out=xw[:, 512:], in_=x_rows[:, 512:])
+        load_scale_rows(nc.sync, ws, w1_scales, range(4))
         nc.sync.dma_start(out=gain[:], in_=gn.rearrange("(p t) o -> p (t o)", t=PACK))
+        nc.sync.dma_start(n1_sb[:], n1)
         nc.sync.dma_start(n2_sb[:], n2)
         nc.sync.dma_start(n3_sb[:], n3)
         nc.sync.dma_start(n4_sb[:], n4)
 
         nc.scalar.activation(gain2[:], gain[:], COPY, scale=0.5)
 
-        def deal(engine, name, words, scales, t0, t1):
+        def deal(engine, name, words, scales, t0, t1, tags=(None, None)):
             n = t1 - t0
-            dw = sb(name + "w", [P, n * 2 * P], U8)
-            ds = sb(name + "s", [P, n * P], U8)
+            dw = sb(name + "w", [P, n * 2 * P], U8, tag=tags[0])
+            ds = sb(name + "s", [P, n * P], U8, tag=tags[1])
             engine.tensor_copy(
                 out=dw[:].rearrange("p (t m b) -> p t m b", t=n, b=2),
                 in_=words[:].rearrange("p (m t b) -> p t m b", t=PACK, b=2)[:, t0:t1],
@@ -102,59 +104,58 @@ def tile_picked_layhopwind_none_po_kernel(tc, x_words, x_scales, w1_words, w1_sc
         xgs = sb("xgs", [P, S], U8)
         xgw = sb("xgw", [P, S], U32, tag="xs")
         nc.vector.tensor_copy(xgs[:], xs[:].indirect(offs_sb[:]))
-        w1 = deal(nc.gpsimd, "w1a", ww, ws, 0, 1)
+        w1 = deal(nc.gpsimd, "w1a", ww, ws, 0, 2)
         for lo, hi in HALVES:
             nc.vector.tensor_copy(xgw[:, lo:hi], xw[:].bitcast(U32).indirect(entries(offs_sb, lo, hi)))
-        w1 = w1 + deal(nc.gpsimd, "w1b", ww, ws, 1, PACK)
+        w1 = w1 + deal(nc.gpsimd, "w1b", ww, ws, 2, PACK)
         nc.sync.dma_start(out=ww[:].bitcast(I32), in_=w2_words[0].bitcast(I32))
         load_scale_rows(nc.sync, ws, w2_scales, range(4))
 
         win = [sb(f"win{t}", [P, S if t == 0 else 2 * S], F32) for t in range(PACK)]
-        st = [sb(f"st{t}", [P, 2 * S if t < 2 else S], F32) for t in range(PACK)]
-        gy = [win[t + 1][:, S:] for t in range(PACK - 1)] + [st[0][:, S:]]
-        stc = [st[1][:, S:]] + [sb(f"stc{t}", [P, S], F32)[:] for t in range(1, PACK)]
+        st = [sb(f"st{t}", [P, S], F32) for t in range(PACK)]
+        gy = [win[t + 1][:, S:] for t in range(PACK - 1)] + [sb("gy3", [P, S], F32)[:]]
+        stc = [sb(f"stc{t}", [P, S], F32) for t in range(PACK)]
         pieces = [(0, 0, S), (1, 0, S)] + [(t, lo, hi) for lo, hi in HALVES for t in (2, 3)]
 
-        nb = 0
+        first = [(t, lo, hi) for lo, hi in HALVES for t in (0, 1)] + [(2, 0, S), (3, 0, S)]
+        for b, (t, lo, hi) in enumerate(first):
+            acc = bank(b)
+            product(acc[:, lo:hi], w1[t], xgw[:, lo:hi], xgs[:, lo:hi])
+            if b == 1:
+                nc.vector.tensor_scalar(win[t][:, lo:hi], acc[:, lo:hi], gain2[:, t : t + 1], None, op0=ALU.mult)
+                nc.vector.tensor_scalar(gy[t][:, lo:hi], acc[:, lo:hi], gain[:, t : t + 1], None, op0=ALU.mult)
+            else:
+                nc.scalar.activation(win[t][:, lo:hi], acc[:, lo:hi], COPY, scale=gain2[:, t : t + 1])
+                nc.scalar.activation(gy[t][:, lo:hi], acc[:, lo:hi], COPY, scale=gain[:, t : t + 1])
         for t in range(PACK):
-            parts = HALVES if t == 0 else [(0, S)]
-            for lo, hi in parts:
-                acc = bank(nb)
-                nb = nb + 1
-                product(acc[:, : hi - lo], w1[t], xgw[:, lo:hi], xgs[:, lo:hi])
-                if lo == 0:
-                    nc.scalar.activation(win[t][:, lo:hi], acc[:, : hi - lo], COPY, scale=gain2[:, t : t + 1])
-                    nc.scalar.activation(gy[t][:, lo:hi], acc[:, : hi - lo], COPY, scale=gain[:, t : t + 1])
-                else:
-                    nc.vector.tensor_scalar(win[t][:, lo:hi], acc[:, : hi - lo], gain2[:, t : t + 1], None, op0=ALU.mult)
-                    nc.vector.tensor_scalar(gy[t][:, lo:hi], acc[:, : hi - lo], gain[:, t : t + 1], None, op0=ALU.mult)
-            for lo, hi in parts:
+            for lo, hi in HALVES if t == 0 else [(0, S)]:
                 nc.vector.tensor_tensor(st[t][:, lo:hi], win[t][:].indirect(entries(n1_sb, lo, hi)), gy[t][:, lo:hi], ALU.add)
-        for t, lo, hi in pieces:
+        for t, lo, hi in [(t, lo, hi) for lo, hi in HALVES for t in range(PACK)]:
             nc.scalar.copy(stc[t][:, lo:hi], st[t][:, lo:hi])
 
         def round_and_interleave(dst, src, lo, hi, scale, split):
-            mid = (lo + hi) // 2 if split else hi
+            mid = lo + 64 if split else hi
             interleave(False, dst[:, : PACK * (mid - lo)], src[:, :, lo:mid], scale)
             if split:
                 interleave(True, dst[:, PACK * (mid - lo) :], src[:, :, mid:hi], scale)
 
-        w2 = deal(nc.vector, "w2a", ww, ws, 0, 2)
+        w2 = deal(nc.vector, "w2a", ww, ws, 0, 2, tags=("win0", "win3"))
         zw = sb("zw", [P, S], U32)
         zs = sb("zs", [P, S], U8)
         h = [win[1], win[2], sb("h2", [P, S], F32), sb("h3", [P, S], F32)]
-        dz = sb("dz", [P, PACK, S], F32)
-        for t, lo, hi in pieces:
-            nc.vector.tensor_tensor(dz[:, t, lo:hi], st[t][:].indirect(entries(n2_sb, lo, hi)), stc[t][:, lo:hi], ALU.subtract)
+        dz = [sb(f"dz{c}", [P, PACK, hi - lo], F32) for c, (lo, hi) in enumerate(HALVES)]
         for c, (lo, hi) in enumerate(HALVES):
-            zb = sb(f"zb{c}", [P, PACK * (hi - lo)], BF16)
-            round_and_interleave(zb, dz, lo, hi, -1.0, c == 1)
+            for t in range(PACK):
+                nc.vector.tensor_tensor(dz[c][:, t, :], st[t][:].indirect(entries(n2_sb, lo, hi)), stc[t][:, lo:hi], ALU.subtract)
+        for c, (lo, hi) in enumerate(HALVES):
+            zb = sb(f"zb{c}", [P, PACK * (hi - lo)], BF16, tag="zb")
+            round_and_interleave(zb, dz[c], 0, hi - lo, -1.0, c == 1)
             nc.vector.quantize_mx(out=zw[:, lo:hi].bitcast(FP8X4), scales=zs[:, lo:hi], in_=zb[:])
             for t in range(2):
-                acc = bank(5 + t if c == 0 else t)
+                acc = bank(6 + t if c == 0 else t)
                 product(acc[:, lo:hi], w2[t], zw[:, lo:hi], zs[:, lo:hi])
                 nc.scalar.copy(h[t][:, lo:hi], acc[:, lo:hi])
-        w2 = w2 + deal(nc.vector, "w2b", ww, ws, 2, PACK)
+        w2 = w2 + deal(nc.vector, "w2b", ww, ws, 2, PACK, tags=("zb", "dz1"))
         for t in range(2, PACK):
             acc = bank(t)
             product(acc[:], w2[t], zw[:], zs[:])

from contextlib import ExitStack

import concourse.mybir as mybir

K, T, S, H, N = 512, 2048, 512, 512, 512
FLOPS = 2 * K * H * S + 2 * H * N * S

F32 = mybir.dt.float32
BF16 = mybir.dt.bfloat16
I32 = mybir.dt.int32
U32 = mybir.dt.uint32
U16 = mybir.dt.uint16
U8 = mybir.dt.uint8
FP8X4 = mybir.dt.float8_e4m3fn_x4
FP4X4 = mybir.dt.float4_e2m1fn_x4
ALU = mybir.AluOpType
COPY = mybir.ActivationFunctionType.Copy

P = 128
PACK = 4
HALVES = [(0, 256), (256, 512)]
CHUNKS = [(0, 256), (256, 384), (384, 512)]


def tile_picked_layhopwind_none_po_kernel(tc, x_words, x_scales, w1_words, w1_scales, gn, w2_words, w2_scales, offs, n1, n2, n3, n4, out_0, out_1, out_2):
    nc = tc.nc
    with ExitStack() as ctx:
        keep = ctx.enter_context(tc.tile_pool(name="keep", bufs=1))
        psum = ctx.enter_context(tc.psum_pool(name="psum", bufs=1))

        def sb(name, shape, dtype, tag=None):
            return keep.tile(shape, dtype, name=name, tag=tag or name, align_bytes=64)

        def bank(b):
            return psum.tile([P, 512], F32, name=f"bank{b}")

        def entries(lst, lo, hi):
            return lst[:, lo // 16 : hi // 16]

        def load_scale_rows(queue, tile, src, quads):
            for q in quads:
                queue.dma_start(out=tile[32 * q : 32 * q + 4, :].bitcast(I32), in_=src[0, 4 * q : 4 * q + 4, :].bitcast(I32))

        offs_sb = keep.tile([P, S // 16], U16, name="offs_sb")
        n1_sb = keep.tile([P, S // 16], U16, name="n1_sb")
        n2_sb = keep.tile([P, S // 16], U16, name="n2_sb")
        n3_sb = keep.tile([P, S // 16], U16, name="n3_sb")
        n4_sb = keep.tile([P, S // 16], U16, name="n4_sb")

        xw = sb("xw", [P, T], I32)
        xs = sb("xs", [P, T], U8)
        ww = sb("ww", [P, 2 * H], U8)
        ws = sb("ws", [P, H], U8)
        gain = sb("gain", [P, PACK], F32)
        gain2 = sb("gain2", [P, PACK], F32)

        nc.vector.memset(xs[:, : T // 2].bitcast(I32), 0)
        nc.gpsimd.memset(xs[:, T // 2 :].bitcast(I32), 0)
        nc.gpsimd.memset(ws[:].bitcast(I32), 0)

        x_rows = x_words[0].rearrange("p n r -> p (n r)").bitcast(I32)
        nc.sync.dma_start(out=xw[:, :512], in_=x_rows[:, :512])
        nc.scalar.dma_start(out=ww[:].bitcast(I32), in_=w1_words[0].bitcast(I32))
        nc.sync.dma_start(offs_sb[:], offs)
        load_scale_rows(nc.sync, xs, x_scales, range(4))
        nc.sync.dma_start(out=xw[:, 512:], in_=x_rows[:, 512:])
        load_scale_rows(nc.sync, ws, w1_scales, range(4))
        nc.sync.dma_start(out=gain[:], in_=gn.rearrange("(p t) o -> p (t o)", t=PACK))
        nc.sync.dma_start(n1_sb[:], n1)
        nc.sync.dma_start(n2_sb[:], n2)
        nc.sync.dma_start(n3_sb[:], n3)
        nc.sync.dma_start(n4_sb[:], n4)

        nc.scalar.activation(gain2[:], gain[:], COPY, scale=0.5)

        def deal(engine, name, words, scales, t0, t1, tags=(None, None)):
            n = t1 - t0
            dw = sb(name + "w", [P, n * 2 * P], U8, tag=tags[0])
            ds = sb(name + "s", [P, n * P], U8, tag=tags[1])
            engine.tensor_copy(
                out=dw[:].rearrange("p (t m b) -> p t m b", t=n, b=2),
                in_=words[:].rearrange("p (m t b) -> p t m b", t=PACK, b=2)[:, t0:t1],
            )
            engine.tensor_copy(
                out=ds[:].rearrange("p (t m) -> p t m", t=n),
                in_=scales[:].rearrange("p (m t) -> p t m", t=PACK)[:, t0:t1],
            )
            return [(dw[:, 2 * P * i : 2 * P * (i + 1)].bitcast(FP4X4), ds[:, P * i : P * (i + 1)]) for i in range(n)]

        def product(dst, weight, words, scales):
            nc.tensor.matmul_mx(out=dst, lhsT=weight[0], lhsT_scale=weight[1], rhs=words.bitcast(FP8X4), rhs_scale=scales, start=True, stop=True)

        def interleave(engine_is_vector, dst, src, scale):
            o = dst.rearrange("p (c i t) -> p c t i", i=4, t=PACK)
            i = src.rearrange("p t (c i) -> p c t i", i=4)
            if engine_is_vector:
                if scale == 1.0:
                    nc.vector.tensor_copy(out=o, in_=i)
                else:
                    nc.vector.tensor_scalar(o, i, scale, None, op0=ALU.mult)
            else:
                nc.scalar.activation(o, i, COPY, scale=scale)

        xgs = sb("xgs", [P, S], U8)
        xgw = sb("xgw", [P, S], U32, tag="xs")
        nc.vector.tensor_copy(xgs[:], xs[:].indirect(offs_sb[:]))
        w1 = deal(nc.gpsimd, "w1a", ww, ws, 0, 2)
        for lo, hi in HALVES:
            nc.vector.tensor_copy(xgw[:, lo:hi], xw[:].bitcast(U32).indirect(entries(offs_sb, lo, hi)))
        w1 = w1 + deal(nc.gpsimd, "w1b", ww, ws, 2, PACK)
        nc.sync.dma_start(out=ww[:].bitcast(I32), in_=w2_words[0].bitcast(I32))
        load_scale_rows(nc.sync, ws, w2_scales, range(4))

        win = [sb(f"win{t}", [P, S if t == 0 else 2 * S], F32) for t in range(PACK)]
        st = [sb(f"st{t}", [P, S], F32) for t in range(PACK)]
        gy = [win[t + 1][:, S:] for t in range(PACK - 1)] + [sb("gy3", [P, S], F32)[:]]
        stc = [sb(f"stc{t}", [P, S], F32) for t in range(PACK)]
        pieces = [(0, 0, S), (1, 0, S)] + [(t, lo, hi) for lo, hi in HALVES for t in (2, 3)]

        first = [(t, lo, hi) for lo, hi in HALVES for t in (0, 1)] + [(2, 0, S), (3, 0, S)]
        for b, (t, lo, hi) in enumerate(first):
            acc = bank(b)
            product(acc[:, lo:hi], w1[t], xgw[:, lo:hi], xgs[:, lo:hi])
            if b == 1:
                nc.vector.tensor_scalar(win[t][:, lo:hi], acc[:, lo:hi], gain2[:, t : t + 1], None, op0=ALU.mult)
                nc.vector.tensor_scalar(gy[t][:, lo:hi], acc[:, lo:hi], gain[:, t : t + 1], None, op0=ALU.mult)
            else:
                nc.scalar.activation(win[t][:, lo:hi], acc[:, lo:hi], COPY, scale=gain2[:, t : t + 1])
                nc.scalar.activation(gy[t][:, lo:hi], acc[:, lo:hi], COPY, scale=gain[:, t : t + 1])
        for t in range(PACK):
            for lo, hi in HALVES if t == 0 else [(0, S)]:
                nc.vector.tensor_tensor(st[t][:, lo:hi], win[t][:].indirect(entries(n1_sb, lo, hi)), gy[t][:, lo:hi], ALU.add)
        for t, lo, hi in [(t, lo, hi) for lo, hi in HALVES for t in range(PACK)]:
            nc.scalar.copy(stc[t][:, lo:hi], st[t][:, lo:hi])

        def round_and_interleave(dst, src, lo, hi, scale, split):
            mid = lo + 64 if split else hi
            interleave(False, dst[:, : PACK * (mid - lo)], src[:, :, lo:mid], scale)
            if split:
                interleave(True, dst[:, PACK * (mid - lo) :], src[:, :, mid:hi], scale)

        w2 = deal(nc.vector, "w2a", ww, ws, 0, 2, tags=("win0", "win3"))
        zw = sb("zw", [P, S], U32)
        zs = sb("zs", [P, S], U8)
        h = [win[1], win[2], sb("h2", [P, S], F32), sb("h3", [P, S], F32)]
        dz = [sb(f"dz{c}", [P, PACK, hi - lo], F32) for c, (lo, hi) in enumerate(HALVES)]
        for c, (lo, hi) in enumerate(HALVES):
            for t in range(PACK):
                nc.vector.tensor_tensor(dz[c][:, t, :], st[t][:].indirect(entries(n2_sb, lo, hi)), stc[t][:, lo:hi], ALU.subtract)
        for c, (lo, hi) in enumerate(HALVES):
            zb = sb(f"zb{c}", [P, PACK * (hi - lo)], BF16, tag="zb")
            round_and_interleave(zb, dz[c], 0, hi - lo, -1.0, c == 1)
            nc.vector.quantize_mx(out=zw[:, lo:hi].bitcast(FP8X4), scales=zs[:, lo:hi], in_=zb[:])
            for t in range(2):
                acc = bank(6 + t if c == 0 else t)
                product(acc[:, lo:hi], w2[t], zw[:, lo:hi], zs[:, lo:hi])
                nc.scalar.copy(h[t][:, lo:hi], acc[:, lo:hi])
        w2 = w2 + deal(nc.vector, "w2b", ww, ws, 2, PACK, tags=("zb", "dz1"))
        for t in range(2, PACK):
            acc = bank(t)
            product(acc[:], w2[t], zw[:], zs[:])
            nc.scalar.copy(h[t][:], acc[:])

        ow = sb("ow", [P, S], U32)
        osc = sb("osc", [P, S], U8)
        out_rows = out_0.rearrange("(p t) j -> p t j", t=PACK)
        out_words = out_1[0].rearrange("p n r -> p (n r)").bitcast(I32)
        g4 = sb("g4", [P, PACK, S], F32)
        dd = sb("dd", [P, PACK, S], F32)
        res = sb("res", [P, PACK, S], F32)
        ob = [sb(f"ob{c}", [P, PACK * (hi - lo)], BF16) for c, (lo, hi) in enumerate(HALVES)]

        def quantise_out(c):
            lo, hi = HALVES[c]
            nc.vector.quantize_mx(out=ow[:, lo:hi].bitcast(FP8X4), scales=osc[:, lo:hi], in_=ob[c][:])
            nc.sync.dma_start(out=out_words[:, lo:hi], in_=ow[:, lo:hi].bitcast(I32))

        for i in range(0, len(pieces), 2):
            pair = pieces[i : i + 2]
            for t, lo, hi in pair:
                nc.vector.tensor_copy(g4[:, t, lo:hi], h[t][:].indirect(entries(n4_sb, lo, hi)))
            for t, lo, hi in pair:
                nc.vector.tensor_tensor(dd[:, t, lo:hi], h[t][:].indirect(entries(n3_sb, lo, hi)), g4[:, t, lo:hi], ALU.subtract)
            if i == 4:
                quantise_out(0)
            for t, lo, hi in pair:
                nc.vector.tensor_tensor(res[:, t, lo:hi], dd[:, t, lo:hi], h[t][:, lo:hi], ALU.mult)
            t0, lo, hi = pair[0]
            nc.sync.dma_start(out=out_rows[:, t0 : t0 + 2, lo:hi], in_=res[:, t0 : t0 + 2, lo:hi])
            if i > 0:
                round_and_interleave(ob[i // 2 - 1], res, lo, hi, 1.0, i == 4)
        quantise_out(1)
        for q in range(4):
            queue = nc.scalar if q < 2 else nc.sync
            queue.dma_start(out=out_2[0, 4 * q : 4 * q + 4, :].bitcast(I32), in_=osc[32 * q : 32 * q + 4, :].bitcast(I32))
